import numpy as np
import ml_dtypes


def mxq(x, axis, fmt="e4m3"):
    dtype, down = {"e4m3": (ml_dtypes.float8_e4m3fn, 7), "e5m2": (ml_dtypes.float8_e5m2, 14)}[fmt]
    v = np.moveaxis(np.asarray(x, np.float32).astype(ml_dtypes.bfloat16).astype(np.float64), axis, -1)
    blocks = v.reshape(v.shape[:-1] + (-1, 32))
    amax = np.abs(blocks).max(-1, keepdims=True)
    byte = np.maximum(np.where(amax > 0, np.frexp(amax)[1] - 1 + 127, 0) - down, 1)
    scale = np.exp2(byte - 127.0)
    codes = (blocks / scale).astype(np.float32).astype(dtype).astype(np.float64)
    return np.moveaxis((codes * scale).reshape(v.shape), -1, axis)


WIDE = False


def mx_kscale(k):
    if not WIDE:
        return np.ones(k)
    levels = np.array([30, -30])
    if k % 512:
        return np.exp2(np.random.permutation(np.resize(levels, k // 32))).repeat(32)
    a = np.empty((k // 512, 16))
    for p in range(k // 512):
        a[p, :8] = np.random.permutation(np.resize(levels, 8))
        for g in range(8):
            far = levels[np.abs(levels - a[p, g]) >= 10]
            a[p, g + 8] = far[np.random.randint(len(far))]
    return np.exp2(a.ravel()).repeat(32)


def f64(x):
    return np.asarray(x).astype(np.float64)


def striped(idx):
    return np.tile(np.asarray(idx).reshape(-1, 16).T, (8, 1)).astype(np.uint16)


def unstriped(offs):
    return offs[:16].T.reshape(-1).astype(np.int64)


E2M1 = np.array([0.0, 0.5, 1.0, 1.5, 2.0, 3.0, 4.0, 6.0, -0.0, -0.5, -1.0, -1.5, -2.0, -3.0, -4.0, -6.0])


def pack_weight(w, fmt):
    k, n = w.shape
    w = f64(np.asarray(w, np.float32).astype(ml_dtypes.bfloat16)).reshape(k // 32, 32, n)
    amax = np.abs(w).max(1)
    if fmt in ("e4m3", "e5m2"):
        byte = np.frexp(amax)[1] - 1 + 127 - (7 if fmt == "e4m3" else 14)
    else:
        mant, ex = np.frexp(amax / 6.0)
        byte = np.where(mant > 0.5, ex, ex - 1) + 127
    byte = np.clip(np.where(amax > 0, byte, 1), 1, 254)
    scaled = (w * np.exp2(127.0 - byte)[:, None, :]).reshape(k, n).astype(np.float32)
    by_word = np.ascontiguousarray(scaled.reshape(k // 512, 128, 4, n).transpose(0, 1, 3, 2))
    if fmt in ("e4m3", "e5m2"):
        words = by_word.astype(ml_dtypes.float8_e4m3fn if fmt == "e4m3" else ml_dtypes.float8_e5m2).view(np.uint8)
    else:
        c = by_word.astype(ml_dtypes.float4_e2m1fn).view(np.uint8) & 0xF
        words = (c[..., 0::2] | (c[..., 1::2] << 4)).reshape(k // 512, 128, 2 * n)
    return np.ascontiguousarray(words), np.ascontiguousarray(byte.astype(np.uint8).reshape(k // 512, 16, n))


def unpack_weight(words, scales, fmt):
    g, _, n = scales.shape
    words = np.ascontiguousarray(words).reshape(g, 128, n, -1)
    if fmt in ("e4m3", "e5m2"):
        vals = words.view(ml_dtypes.float8_e4m3fn if fmt == "e4m3" else ml_dtypes.float8_e5m2).astype(np.float64)
    else:
        nib = np.empty((g, 128, n, 4), np.uint8)
        nib[..., 0::2] = words & 0xF
        nib[..., 1::2] = words >> 4
        vals = E2M1[nib]
    vals = vals * np.repeat(np.exp2(scales.astype(np.float64) - 127.0), 8, axis=1)[..., None]
    return vals.transpose(0, 1, 3, 2).reshape(g * 512, n)


K, F, T, Z, J, R, C, N, E = 512, 512, 1024, 1024, 256, 512, 512, 256, 1024


def setup_inputs():
    n = np.random.standard_normal
    idx = np.random.permutation(T)[:J]
    idx2 = np.random.permutation(Z)[:J]
    idx3 = np.random.permutation(C)[:J]
    idx4 = np.random.permutation(C)[:J]
    idx5 = np.random.permutation(E)[:J]
    fk = mx_kscale(K)
    fr = mx_kscale(R)
    ff = mx_kscale(F)
    xtp = pack_weight(n((K, T)) / fk[:, None], "e4m3")
    wp = pack_weight(n((K, R)) * 1 / np.sqrt(K) * fk[:, None] * fr, "e2m1")
    xop = pack_weight(n((F, Z)) / ff[:, None], "e2m1")
    w0p = pack_weight(n((F, R)) * 1 / np.sqrt(F) * ff[:, None] * fr, "e5m2")
    wbp = pack_weight(n((R, N)) * 1 / np.sqrt(R) / fr[:, None], "e5m2")
    return {
        "xt_words": xtp[0],
        "xt_scales": xtp[1],
        "w_words": wp[0],
        "w_scales": wp[1],
        "xo_words": xop[0],
        "xo_scales": xop[1],
        "w0_words": w0p[0],
        "w0_scales": w0p[1],
        "sa": (np.random.uniform(0.5, 1.6, (R, 1))).astype(np.float32),
        "wb_words": wbp[0],
        "wb_scales": wbp[1],
        "tz": (np.random.randint(-9, 10, (N, E)).astype(np.float64)).astype(np.float32),
        "so": (np.random.uniform(0.1, 0.3, (N, 1))).astype(np.float32),
        "offs": striped(idx),
        "offs2": striped(idx2),
        "offs3": striped(idx3),
        "offs4": striped(idx4),
        "offs5": striped(idx5),
    }


def reference(xt_words, xt_scales, w_words, w_scales, xo_words, xo_scales, w0_words, w0_scales, sa, wb_words, wb_scales, tz, so, offs, offs2, offs3, offs4, offs5):
    idx = unstriped(offs)
    idx2 = unstriped(offs2)
    idx3 = unstriped(offs3)
    idx4 = unstriped(offs4)
    idx5 = unstriped(offs5)
    xtu = unpack_weight(xt_words, xt_scales, "e4m3")
    wu = unpack_weight(w_words, w_scales, "e2m1")
    xou = unpack_weight(xo_words, xo_scales, "e2m1")
    w0u = unpack_weight(w0_words, w0_scales, "e5m2")
    wbu = unpack_weight(wb_words, wb_scales, "e5m2")
    xtidxg = xtu[:, idx]
    xoidx2g = xou[:, idx2]
    a = wu.T @ xtidxg + w0u.T @ xoidx2g
    pw = np.zeros((R, C))
    pw[:, idx3] = a
    hid = np.abs(pw[:, idx4] * f64(sa) - a)
    hidq = mxq(hid, 0, "e4m3")
    p = wbu.T @ hidq
    y = np.maximum(p, f64(tz)[:, idx5] * f64(so))
    return y

@@ -1,0 +1,165 @@
+from contextlib import ExitStack
+
+import concourse.mybir as mybir
+
+K, F, T, Z, J, R, C, N, E = 512, 512, 1024, 1024, 256, 512, 512, 256, 1024
+FLOPS = 2 * J * (K * R + F * R + R * N)
+
+F32 = mybir.dt.float32
+BF16 = mybir.dt.bfloat16
+I32 = mybir.dt.int32
+U32 = mybir.dt.uint32
+U16 = mybir.dt.uint16
+U8 = mybir.dt.uint8
+E4M3 = mybir.dt.float8_e4m3fn_x4
+E5M2 = mybir.dt.float8_e5m2_x4
+E2M1 = mybir.dt.float4_e2m1fn_x4
+ACT = mybir.ActivationFunctionType
+ALU = mybir.AluOpType
+
+P = 128
+PACK = 4
+HALF = J // 2
+COLS = J // 16
+VECTOR_SHARE = 6
+
+
+def tile_list_boardownweighed_bank_one_stepfloor_kernel(
+    tc, xt_words, xt_scales, w_words, w_scales, xo_words, xo_scales, w0_words, w0_scales,
+    sa, wb_words, wb_scales, tz, so, offs, offs2, offs3, offs4, offs5, out,
+):
+    nc = tc.nc
+    with ExitStack() as ctx:
+        lists = ctx.enter_context(tc.tile_pool(name="lists", bufs=1))
+        sb = ctx.enter_context(tc.tile_pool(name="sb", bufs=1))
+        psum = ctx.enter_context(tc.psum_pool(name="psum", bufs=1))
+
+        def tile(shape, dtype, name, tag=None):
+            return sb.tile(shape, dtype, name=name, tag=tag or name, align_bytes=64)
+
+        idx = [lists.tile([P, COLS], U16, name=f"idx{i}") for i in range(5)]
+        xt_tab = tile([P, T], U32, "xt_tab")
+        xo_tab = tile([P, Z], U16, "xo_tab")
+        xt_stage = tile([P // 2, 2, T], U8, "xt_stage")
+        xo_stage = tile([P // 2, 2, Z], U8, "xo_stage")
+        xt_sc = tile([P, T], U8, "xt_sc")
+        xo_sc = tile([P, Z], U8, "xo_sc")
+        w_raw = tile([P, R], U16, "w_raw")
+        w0_raw = tile([P, R], U32, "w0_raw")
+        wsc_raw = tile([P, 2, 2, R], U8, "wsc_raw")
+        wb_tab = tile([P, N], U32, "wb_tab")
+        wb_sc = tile([P, N], U8, "wb_sc")
+        tz_tab = [tile([P, E], F32, f"tz{h}") for h in range(2)]
+        sa_t = tile([P, PACK], F32, "sa_t")
+        so_t = tile([P, 2], F32, "so_t")
+        board = [tile([P, C], F32, f"board{t}") for t in range(PACK)]
+
+        nc.vector.memset(xt_stage[:].bitcast(I32), 0)
+        nc.vector.memset(xo_stage[:].bitcast(I32), 0)
+        nc.vector.memset(wsc_raw[:].bitcast(I32), 0)
+        nc.vector.memset(wb_sc[:].bitcast(I32), 0)
+        for t in range(PACK):
+            nc.vector.memset(board[t][:], 0.0)
+
+        def load_scale_pairs(dst, scales):
+            rows = scales[0].bitcast(I32).rearrange("(c h r) n -> h r c n", c=2, h=2)
+            for h in range(2):
+                nc.sync.dma_start(dst(h), rows[h])
+
+        nc.sync.dma_start(idx[0][:], offs)
+        nc.sync.dma_start(idx[1][:], offs2)
+        load_scale_pairs(lambda h: xt_stage[32 * h : 32 * h + 4].bitcast(I32), xt_scales)
+        load_scale_pairs(lambda h: xo_stage[32 * h : 32 * h + 4].bitcast(I32), xo_scales)
+        nc.sync.dma_start(xt_tab[:].bitcast(I32), xt_words[0].rearrange("p n t -> p (n t)").bitcast(I32))
+        nc.sync.dma_start(xo_tab[:].bitcast(I32), xo_words[0].bitcast(I32))
+        nc.sync.dma_start(w_raw[:].bitcast(I32), w_words[0].bitcast(I32))
+        nc.sync.dma_start(w0_raw[:].bitcast(I32), w0_words[0].rearrange("p n t -> p (n t)").bitcast(I32))
+        load_scale_pairs(lambda h: wsc_raw[32 * h : 32 * h + 4, :, 0, :].bitcast(I32), w_scales)
+        load_scale_pairs(lambda h: wsc_raw[32 * h : 32 * h + 4, :, 1, :].bitcast(I32), w0_scales)
+        nc.sync.dma_start(tz_tab[0][:], tz[0:P, :])
+        nc.sync.dma_start(idx[2][:], offs3)
+        nc.sync.dma_start(idx[4][:], offs5)
+        with nc.allow_non_contiguous_dma(reason="one value a partition and half"):
+            nc.sync.dma_start(so_t[:], so.rearrange("(h p) o -> p (h o)", h=2))
+        nc.sync.dma_start(idx[3][:], offs4)
+        nc.sync.dma_start(sa_t[:], sa.rearrange("(p t) o -> p (t o)", t=PACK))
+        nc.sync.dma_start(tz_tab[1][:], tz[P : 2 * P, :])
+        nc.sync.dma_start(wb_tab[:].bitcast(I32), wb_words[0].rearrange("p n t -> p (n t)").bitcast(I32))
+        for q in range(4):
+            nc.sync.dma_start(wb_sc[32 * q : 32 * q + 4, :].bitcast(I32), wb_scales[0, 4 * q : 4 * q + 4, :].bitcast(I32))
+
+        xt_g = tile([P, J], U32, "xt_g")
+        xt_gs = tile([P, J], U8, "xt_gs")
+        xo_g = tile([P, J], U16, "xo_g")
+        xo_gs = tile([P, J], U8, "xo_gs")
+        for stage, plane, got, lst in ((xt_stage, xt_sc, xt_gs, idx[0]), (xo_stage, xo_sc, xo_gs, idx[1])):
+            for c in range(2):
+                nc.vector.tensor_copy(plane[64 * c : 64 * c + 64, :].bitcast(I32), stage[:, c, :].bitcast(I32))
+            nc.vector.tensor_copy(got[:], plane[:].indirect(lst[:]))
+        nc.vector.tensor_copy(xt_g[:], xt_tab[:].indirect(idx[0][:]))
+        nc.vector.tensor_copy(xo_g[:], xo_tab[:].indirect(idx[1][:]))
+
+        w_t = tile([P, PACK, P], U16, "w_t")
+        w0_t = tile([P, PACK, P], U32, "w0_t")
+        nc.scalar.copy(w_t[:].rearrange("p t (b i) -> p b t i", i=8), w_raw[:].rearrange("p (b i t) -> p b t i", i=8, t=PACK))
+        nc.scalar.copy(w0_t[:].rearrange("p t (b i) -> p b t i", i=4), w0_raw[:].rearrange("p (b i t) -> p b t i", i=4, t=PACK))
+
+        nc.vector.tensor_copy(
+            wsc_raw[64:128, 0].rearrange("p m n -> p (m n)").bitcast(I32),
+            wsc_raw[0:64, 1].rearrange("p m n -> p (m n)").bitcast(I32),
+        )
+        wsc_t = [tile([P, 2 * P], U8, f"wsc_t{t}") for t in range(PACK)]
+        acc = [psum.tile([P, J], F32, name=f"acc{t}") for t in range(PACK)]
+        for t in range(PACK):
+            nc.vector.tensor_copy(wsc_t[t][:], wsc_raw[:, 0].rearrange("p m (q t) -> p t (m q)", t=PACK)[:, t, :])
+            nc.tensor.matmul_mx(acc[t][:], lhsT=w_t[:, t, :].bitcast(E2M1), lhsT_scale=wsc_t[t][:, 0:P],
+                                rhs=xt_g[:].bitcast(E4M3), rhs_scale=xt_gs[:], start=True, stop=False)
+            nc.tensor.matmul_mx(acc[t][:], lhsT=w0_t[:, t, :].bitcast(E5M2), lhsT_scale=wsc_t[t][:, P : 2 * P],
+                                rhs=xo_g[:].bitcast(E2M1), rhs_scale=xo_gs[:], start=False, stop=True)
+
+        floor0 = tile([P, J], F32, "floor0")
+        nc.scalar.activation(floor0[:], tz_tab[0][:].indirect(idx[4][:]), ACT.Copy, scale=so_t[:, 0:1])
+
+        a = [tile([P, J], F32, f"a{t}", tag="late" if t == 3 else None) for t in range(PACK)]
+        s = VECTOR_SHARE
+        nc.vector.tensor_copy(a[0][:], acc[0][:])
+        nc.vector.tensor_copy(board[0][:].indirect(idx[2][:]), a[0][:])
+        nc.scalar.copy(a[1][:], acc[1][:])
+        nc.scalar.activation(board[1][:].indirect(idx[2][:]), a[1][:], ACT.Copy)
+        nc.vector.tensor_copy(a[2][:], acc[2][:])
+        nc.vector.tensor_copy(board[2][:].indirect(idx[2][:, 0:s]), a[2][:, 0 : 16 * s])
+        nc.scalar.activation(board[2][:].indirect(idx[2][:, s:COLS]), a[2][:, 16 * s : J], ACT.Copy)
+        nc.vector.tensor_copy(a[3][:], acc[3][:])
+        nc.vector.tensor_copy(board[3][:].indirect(idx[2][:]), a[3][:])
+
+        read = [tile([P, J], F32, f"read{t}") for t in range(PACK)]
+        diff = tile([P, 2, PACK, HALF], F32, "diff", tag="late")
+        for t in range(PACK - 1):
+            nc.scalar.activation(read[t][:], board[t][:].indirect(idx[3][:]), ACT.Copy, scale=sa_t[:, t : t + 1])
+            nc.vector.tensor_tensor(diff[:, :, t, :], read[t][:].rearrange("p (u j) -> p u j", u=2),
+                                    a[t][:].rearrange("p (u j) -> p u j", u=2), ALU.subtract)
+        for u in range(2):
+            cols = slice(u * HALF, (u + 1) * HALF)
+            nc.scalar.activation(read[3][:, cols], board[3][:].indirect(idx[3][:, 8 * u : 8 * u + 8]),
+                                 ACT.Copy, scale=sa_t[:, 3:4])
+            nc.vector.tensor_tensor(diff[:, u, 3, :], read[3][:, cols], acc[3][:, cols], ALU.subtract)
+
+        prod = [psum.tile([P, J], F32, name=f"prod{h}") for h in range(2)]
+        for u in range(2):
+            hid = tile([P, HALF * PACK], BF16, f"hid{u}")
+            nc.scalar.activation(hid[:].rearrange("p (c i t) -> p c t i", i=4, t=PACK),
+                                 diff[:, u].rearrange("p t (c i) -> p c t i", i=4), ACT.Abs)
+            hq = tile([P, HALF], U32, f"hq{u}")
+            hs = tile([P, HALF], U8, f"hs{u}")
+            nc.vector.quantize_mx(hq[:].bitcast(E4M3), hs[:], hid[:])
+            for h in range(2):
+                nc.tensor.matmul_mx(prod[h][:, u * HALF : (u + 1) * HALF], lhsT=wb_tab[:, h * P : (h + 1) * P].bitcast(E5M2),
+                                    lhsT_scale=wb_sc[:, h * P : (h + 1) * P], rhs=hq[:].bitcast(E4M3), rhs_scale=hs[:],
+                                    start=True, stop=True)
+
+        floor1 = tile([P, J], F32, "floor1", tag="late")
+        nc.scalar.activation(floor1[:], tz_tab[1][:].indirect(idx[4][:]), ACT.Copy, scale=so_t[:, 1:2])
+        for h, floor in enumerate((floor0, floor1)):
+            y = tile([P, J], F32, f"y{h}")
+            nc.vector.tensor_tensor(y[:], prod[h][:], floor[:], ALU.max)
+            nc.sync.dma_start(out[h * P : (h + 1) * P, :], y[:])

@@ -21,7 +21,8 @@ P = 128
 PACK = 4
 HALF = J // 2
 COLS = J // 16
-VECTOR_SHARE = 6
+SHARE = 4
+ABS_VECTOR = 64
 
 
 def tile_list_boardownweighed_bank_one_stepfloor_kernel(
@@ -40,13 +41,13 @@ def tile_list_boardownweighed_bank_one_stepfloor_kernel(
         idx = [lists.tile([P, COLS], U16, name=f"idx{i}") for i in range(5)]
         xt_tab = tile([P, T], U32, "xt_tab")
         xo_tab = tile([P, Z], U16, "xo_tab")
-        xt_stage = tile([P // 2, 2, T], U8, "xt_stage")
-        xo_stage = tile([P // 2, 2, Z], U8, "xo_stage")
+        xo_fold = tile([P // 2, 2, Z], U8, "xo_fold")
         xt_sc = tile([P, T], U8, "xt_sc")
         xo_sc = tile([P, Z], U8, "xo_sc")
         w_raw = tile([P, R], U16, "w_raw")
         w0_raw = tile([P, R], U32, "w0_raw")
-        wsc_raw = tile([P, 2, 2, R], U8, "wsc_raw")
+        wsc_raw = tile([P, 2, R], U8, "wsc_raw")
+        w0sc_raw = tile([P, 2, R], U8, "w0sc_raw")
         wb_tab = tile([P, N], U32, "wb_tab")
         wb_sc = tile([P, N], U8, "wb_sc")
         tz_tab = [tile([P, E], F32, f"tz{h}") for h in range(2)]
@@ -54,101 +55,105 @@ def tile_list_boardownweighed_bank_one_stepfloor_kernel(
         so_t = tile([P, 2], F32, "so_t")
         board = [tile([P, C], F32, f"board{t}") for t in range(PACK)]
 
-        nc.vector.memset(xt_stage[:].bitcast(I32), 0)
-        nc.vector.memset(xo_stage[:].bitcast(I32), 0)
-        nc.vector.memset(wsc_raw[:].bitcast(I32), 0)
-        nc.vector.memset(wb_sc[:].bitcast(I32), 0)
+        for plane in (xo_fold, w0sc_raw, xt_sc, wsc_raw, wb_sc):
+            nc.vector.memset(plane[:].bitcast(I32), 0)
         for t in range(PACK):
             nc.vector.memset(board[t][:], 0.0)
 
-        def load_scale_pairs(dst, scales):
+        def load_plane(plane, scales):
+            for q in range(4):
+                nc.sync.dma_start(plane[32 * q : 32 * q + 4, :].bitcast(I32), scales[0, 4 * q : 4 * q + 4, :].bitcast(I32))
+
+        def load_plane_folded(queue, folded, scales):
             rows = scales[0].bitcast(I32).rearrange("(c h r) n -> h r c n", c=2, h=2)
             for h in range(2):
-                nc.sync.dma_start(dst(h), rows[h])
+                queue.dma_start(folded[32 * h : 32 * h + 4].bitcast(I32), rows[h])
 
-        nc.sync.dma_start(idx[0][:], offs)
+        def load_words(tab, words):
+            nc.sync.dma_start(tab[:].bitcast(I32), words.bitcast(I32))
+
         nc.sync.dma_start(idx[1][:], offs2)
-        load_scale_pairs(lambda h: xt_stage[32 * h : 32 * h + 4].bitcast(I32), xt_scales)
-        load_scale_pairs(lambda h: xo_stage[32 * h : 32 * h + 4].bitcast(I32), xo_scales)
-        nc.sync.dma_start(xt_tab[:].bitcast(I32), xt_words[0].rearrange("p n t -> p (n t)").bitcast(I32))
-        nc.sync.dma_start(xo_tab[:].bitcast(I32), xo_words[0].bitcast(I32))
-        nc.sync.dma_start(w_raw[:].bitcast(I32), w_words[0].bitcast(I32))
-        nc.sync.dma_start(w0_raw[:].bitcast(I32), w0_words[0].rearrange("p n t -> p (n t)").bitcast(I32))
-        load_scale_pairs(lambda h: wsc_raw[32 * h : 32 * h + 4, :, 0, :].bitcast(I32), w_scales)
-        load_scale_pairs(lambda h: wsc_raw[32 * h : 32 * h + 4, :, 1, :].bitcast(I32), w0_scales)
-        nc.sync.dma_start(tz_tab[0][:], tz[0:P, :])
+        nc.sync.dma_start(idx[0][:], offs)
+        load_words(xo_tab, xo_words[0])
+        load_plane_folded(nc.sync, xo_fold, xo_scales)
+        load_words(w0_raw, w0_words[0].rearrange("p n t -> p (n t)"))
+        load_plane_folded(nc.sync, w0sc_raw, w0_scales)
+        load_words(xt_tab, xt_words[0].rearrange("p n t -> p (n t)"))
+        load_words(w_raw, w_words[0])
+        load_plane(xt_sc, xt_scales)
+        load_plane_folded(nc.sync, wsc_raw, w_scales)
         nc.sync.dma_start(idx[2][:], offs3)
+        nc.sync.dma_start(idx[3][:], offs4)
+        nc.sync.dma_start(sa_t[:], sa.rearrange("(p t) o -> p (t o)", t=PACK))
+        load_words(wb_tab, wb_words[0].rearrange("p n t -> p (n t)"))
+        load_plane(wb_sc, wb_scales)
         nc.sync.dma_start(idx[4][:], offs5)
         with nc.allow_non_contiguous_dma(reason="one value a partition and half"):
             nc.sync.dma_start(so_t[:], so.rearrange("(h p) o -> p (h o)", h=2))
-        nc.sync.dma_start(idx[3][:], offs4)
-        nc.sync.dma_start(sa_t[:], sa.rearrange("(p t) o -> p (t o)", t=PACK))
-        nc.sync.dma_start(tz_tab[1][:], tz[P : 2 * P, :])
-        nc.sync.dma_start(wb_tab[:].bitcast(I32), wb_words[0].rearrange("p n t -> p (n t)").bitcast(I32))
-        for q in range(4):
-            nc.sync.dma_start(wb_sc[32 * q : 32 * q + 4, :].bitcast(I32), wb_scales[0, 4 * q : 4 * q + 4, :].bitcast(I32))
+        for h in range(2):
+            nc.sync.dma_start(tz_tab[h][:], tz[h * P : (h + 1) * P, :])
 
         xt_g = tile([P, J], U32, "xt_g")
         xt_gs = tile([P, J], U8, "xt_gs")
         xo_g = tile([P, J], U16, "xo_g")
         xo_gs = tile([P, J], U8, "xo_gs")
-        for stage, plane, got, lst in ((xt_stage, xt_sc, xt_gs, idx[0]), (xo_stage, xo_sc, xo_gs, idx[1])):
-            for c in range(2):
-                nc.vector.tensor_copy(plane[64 * c : 64 * c + 64, :].bitcast(I32), stage[:, c, :].bitcast(I32))
-            nc.vector.tensor_copy(got[:], plane[:].indirect(lst[:]))
-        nc.vector.tensor_copy(xt_g[:], xt_tab[:].indirect(idx[0][:]))
-        nc.vector.tensor_copy(xo_g[:], xo_tab[:].indirect(idx[1][:]))
-
         w_t = tile([P, PACK, P], U16, "w_t")
         w0_t = tile([P, PACK, P], U32, "w0_t")
-        nc.scalar.copy(w_t[:].rearrange("p t (b i) -> p b t i", i=8), w_raw[:].rearrange("p (b i t) -> p b t i", i=8, t=PACK))
-        nc.scalar.copy(w0_t[:].rearrange("p t (b i) -> p b t i", i=4), w0_raw[:].rearrange("p (b i t) -> p b t i", i=4, t=PACK))
-
-        nc.vector.tensor_copy(
-            wsc_raw[64:128, 0].rearrange("p m n -> p (m n)").bitcast(I32),
-            wsc_raw[0:64, 1].rearrange("p m n -> p (m n)").bitcast(I32),
-        )
-        wsc_t = [tile([P, 2 * P], U8, f"wsc_t{t}") for t in range(PACK)]
+        w0sc_t = tile([P, PACK, P], U8, "w0sc_t")
+        wsc_t = [tile([P, P], U8, f"wsc_t{t}") for t in range(PACK)]
         acc = [psum.tile([P, J], F32, name=f"acc{t}") for t in range(PACK)]
+
+        nc.vector.tensor_copy(xo_g[:], xo_tab[:].indirect(idx[1][:]))
+        for c in range(2):
+            nc.vector.tensor_copy(xo_sc[64 * c : 64 * c + 64, :].bitcast(I32), xo_fold[:, c, :].bitcast(I32))
+        nc.vector.tensor_copy(xo_gs[:], xo_sc[:].indirect(idx[1][:]))
+        nc.scalar.copy(w0_t[:].rearrange("p t (b i) -> p b t i", i=4), w0_raw[:].rearrange("p (b i t) -> p b t i", i=4, t=PACK))
+        nc.vector.tensor_copy(w0sc_raw[64:128, 0, :].bitcast(I32), w0sc_raw[0:64, 1, :].bitcast(I32))
+        nc.vector.tensor_copy(w0sc_t[:].rearrange("p t (b i) -> p b t i", i=16),
+                              w0sc_raw[:, 0, :].rearrange("p (b i t) -> p b t i", i=16, t=PACK))
         for t in range(PACK):
-            nc.vector.tensor_copy(wsc_t[t][:], wsc_raw[:, 0].rearrange("p m (q t) -> p t (m q)", t=PACK)[:, t, :])
-            nc.tensor.matmul_mx(acc[t][:], lhsT=w_t[:, t, :].bitcast(E2M1), lhsT_scale=wsc_t[t][:, 0:P],
-                                rhs=xt_g[:].bitcast(E4M3), rhs_scale=xt_gs[:], start=True, stop=False)
-            nc.tensor.matmul_mx(acc[t][:], lhsT=w0_t[:, t, :].bitcast(E5M2), lhsT_scale=wsc_t[t][:, P : 2 * P],
-                                rhs=xo_g[:].bitcast(E2M1), rhs_scale=xo_gs[:], start=False, stop=True)
+            nc.tensor.matmul_mx(acc[t][:], lhsT=w0_t[:, t, :].bitcast(E5M2), lhsT_scale=w0sc_t[:, t, :],
+                                rhs=xo_g[:].bitcast(E2M1), rhs_scale=xo_gs[:], start=True, stop=False)
 
-        floor0 = tile([P, J], F32, "floor0")
-        nc.scalar.activation(floor0[:], tz_tab[0][:].indirect(idx[4][:]), ACT.Copy, scale=so_t[:, 0:1])
+        nc.vector.tensor_copy(xt_g[:], xt_tab[:].indirect(idx[0][:]))
+        nc.vector.tensor_copy(xt_gs[:], xt_sc[:].indirect(idx[0][:]))
+        nc.scalar.copy(w_t[:].rearrange("p t (b i) -> p b t i", i=8), w_raw[:].rearrange("p (b i t) -> p b t i", i=8, t=PACK))
+        nc.vector.tensor_copy(wsc_raw[64:128, 0, :].bitcast(I32), wsc_raw[0:64, 1, :].bitcast(I32))
+        for t in range(PACK):
+            nc.vector.tensor_copy(wsc_t[t][:], wsc_raw[:, 0, :].rearrange("p (q t) -> p t q", t=PACK)[:, t, :])
+            nc.tensor.matmul_mx(acc[t][:], lhsT=w_t[:, t, :].bitcast(E2M1), lhsT_scale=wsc_t[t][:],
+                                rhs=xt_g[:].bitcast(E4M3), rhs_scale=xt_gs[:], start=False, stop=True)
 
-        a = [tile([P, J], F32, f"a{t}", tag="late" if t == 3 else None) for t in range(PACK)]
-        s = VECTOR_SHARE
-        nc.vector.tensor_copy(a[0][:], acc[0][:])
-        nc.vector.tensor_copy(board[0][:].indirect(idx[2][:]), a[0][:])
-        nc.scalar.copy(a[1][:], acc[1][:])
-        nc.scalar.activation(board[1][:].indirect(idx[2][:]), a[1][:], ACT.Copy)
-        nc.vector.tensor_copy(a[2][:], acc[2][:])
-        nc.vector.tensor_copy(board[2][:].indirect(idx[2][:, 0:s]), a[2][:, 0 : 16 * s])
-        nc.scalar.activation(board[2][:].indirect(idx[2][:, s:COLS]), a[2][:, 16 * s : J], ACT.Copy)
-        nc.vector.tensor_copy(a[3][:], acc[3][:])
-        nc.vector.tensor_copy(board[3][:].indirect(idx[2][:]), a[3][:])
-
-        read = [tile([P, J], F32, f"read{t}") for t in range(PACK)]
-        diff = tile([P, 2, PACK, HALF], F32, "diff", tag="late")
-        for t in range(PACK - 1):
-            nc.scalar.activation(read[t][:], board[t][:].indirect(idx[3][:]), ACT.Copy, scale=sa_t[:, t : t + 1])
-            nc.vector.tensor_tensor(diff[:, :, t, :], read[t][:].rearrange("p (u j) -> p u j", u=2),
-                                    a[t][:].rearrange("p (u j) -> p u j", u=2), ALU.subtract)
+        a = [tile([P, J], F32, f"a{t}", tag={2: "vector_slot", 3: "scalar_slot"}.get(t)) for t in range(PACK)]
+        cut = 16 * SHARE
+        for t in range(PACK):
+            nc.scalar.copy(a[t][:], acc[t][:])
+        for t in range(2):
+            nc.vector.tensor_copy(board[t][:].indirect(idx[2][:]), a[t][:])
+        nc.scalar.activation(board[2][:].indirect(idx[2][:, 0:SHARE]), a[2][:, 0:cut], ACT.Copy)
+        nc.vector.tensor_copy(board[2][:].indirect(idx[2][:, SHARE:COLS]), a[2][:, cut:J])
+        nc.scalar.activation(board[3][:].indirect(idx[2][:]), a[3][:], ACT.Copy)
+        read = tile([P, PACK, J], F32, "read", tag="scalar_slot")
+        for t in (0, 3, 1):
+            nc.scalar.activation(read[:, t, :], board[t][:].indirect(idx[3][:]), ACT.Copy, scale=sa_t[:, t : t + 1])
+        diff = tile([P, 2, PACK, HALF], F32, "diff", tag="vector_slot")
         for u in range(2):
             cols = slice(u * HALF, (u + 1) * HALF)
-            nc.scalar.activation(read[3][:, cols], board[3][:].indirect(idx[3][:, 8 * u : 8 * u + 8]),
-                                 ACT.Copy, scale=sa_t[:, 3:4])
-            nc.vector.tensor_tensor(diff[:, u, 3, :], read[3][:, cols], acc[3][:, cols], ALU.subtract)
+            nc.scalar.activation(read[:, 2, cols], board[2][:].indirect(idx[3][:, 8 * u : 8 * u + 8]),
+                                 ACT.Copy, scale=sa_t[:, 2:3])
+            for t in (0, 3, 1, 2):
+                nc.vector.tensor_tensor(diff[:, u, t, :], read[:, t, cols], acc[t][:, cols], ALU.subtract)
 
         prod = [psum.tile([P, J], F32, name=f"prod{h}") for h in range(2)]
         for u in range(2):
             hid = tile([P, HALF * PACK], BF16, f"hid{u}")
-            nc.scalar.activation(hid[:].rearrange("p (c i t) -> p c t i", i=4, t=PACK),
-                                 diff[:, u].rearrange("p t (c i) -> p c t i", i=4), ACT.Abs)
+            n_scalar = HALF if u == 0 else HALF - ABS_VECTOR
+            nc.scalar.activation(hid[:, 0 : n_scalar * PACK].rearrange("p (c i t) -> p c t i", i=4, t=PACK),
+                                 diff[:, u, :, 0:n_scalar].rearrange("p t (c i) -> p c t i", i=4), ACT.Abs)
+            if u == 1:
+                rest = diff[:, u, :, n_scalar:HALF].rearrange("p t j -> p j t")
+                nc.vector.scalar_tensor_tensor(hid[:, n_scalar * PACK :].rearrange("p (j t) -> p j t", t=PACK),
+                                               rest, -1.0, rest, ALU.mult, ALU.max)
             hq = tile([P, HALF], U32, f"hq{u}")
             hs = tile([P, HALF], U8, f"hs{u}")
             nc.vector.quantize_mx(hq[:].bitcast(E4M3), hs[:], hid[:])
@@ -157,9 +162,9 @@ def tile_list_boardownweighed_bank_one_stepfloor_kernel(
                                     lhsT_scale=wb_sc[:, h * P : (h + 1) * P], rhs=hq[:].bitcast(E4M3), rhs_scale=hs[:],
                                     start=True, stop=True)
 
-        floor1 = tile([P, J], F32, "floor1", tag="late")
-        nc.scalar.activation(floor1[:], tz_tab[1][:].indirect(idx[4][:]), ACT.Copy, scale=so_t[:, 1:2])
-        for h, floor in enumerate((floor0, floor1)):
+        floor = tile([P, 2, J], F32, "floor", tag="vector_slot")
+        for h in range(2):
+            nc.scalar.activation(floor[:, h, :], tz_tab[h][:].indirect(idx[4][:]), ACT.Copy, scale=so_t[:, h : h + 1])
             y = tile([P, J], F32, f"y{h}")
-            nc.vector.tensor_tensor(y[:], prod[h][:], floor[:], ALU.max)
+            nc.vector.tensor_tensor(y[:], prod[h][:], floor[:, h, :], ALU.max)
             nc.sync.dma_start(out[h * P : (h + 1) * P, :], y[:])

@@ -19,9 +19,12 @@ ALU = mybir.AluOpType
 
 P = 128
 PACK = 4
+QUAD = 32
 HALF = J // 2
-COLS = J // 16
-SHARE = 4
+LIST_COLS = J // 16
+SPLIT_SLICE = 2
+SCALAR_SLICE = 3
+SCALAR_SHARE = 4
 ABS_VECTOR = 64
 
 
@@ -38,7 +41,9 @@ def tile_list_boardownweighed_bank_one_stepfloor_kernel(
         def tile(shape, dtype, name, tag=None):
             return sb.tile(shape, dtype, name=name, tag=tag or name, align_bytes=64)
 
-        idx = [lists.tile([P, COLS], U16, name=f"idx{i}") for i in range(5)]
+        token_list, note_list, put_list, read_list, floor_list = [
+            lists.tile([P, LIST_COLS], U16, name=f"list{i}") for i in range(5)
+        ]
         xt_tab = tile([P, T], U32, "xt_tab")
         xo_tab = tile([P, Z], U16, "xo_tab")
         xo_fold = tile([P // 2, 2, Z], U8, "xo_fold")
@@ -46,8 +51,8 @@ def tile_list_boardownweighed_bank_one_stepfloor_kernel(
         xo_sc = tile([P, Z], U8, "xo_sc")
         w_raw = tile([P, R], U16, "w_raw")
         w0_raw = tile([P, R], U32, "w0_raw")
-        wsc_raw = tile([P, 2, R], U8, "wsc_raw")
-        w0sc_raw = tile([P, 2, R], U8, "w0sc_raw")
+        wsc_fold = tile([P, 2, R], U8, "wsc_fold")
+        w0sc_fold = tile([P, 2, R], U8, "w0sc_fold")
         wb_tab = tile([P, N], U32, "wb_tab")
         wb_sc = tile([P, N], U8, "wb_sc")
         tz_tab = [tile([P, E], F32, f"tz{h}") for h in range(2)]
@@ -55,40 +60,40 @@ def tile_list_boardownweighed_bank_one_stepfloor_kernel(
         so_t = tile([P, 2], F32, "so_t")
         board = [tile([P, C], F32, f"board{t}") for t in range(PACK)]
 
-        for plane in (xo_fold, w0sc_raw, xt_sc, wsc_raw, wb_sc):
+        for plane in (xo_fold, w0sc_fold, xt_sc, wsc_fold, wb_sc):
             nc.vector.memset(plane[:].bitcast(I32), 0)
         for t in range(PACK):
-            nc.vector.memset(board[t][:], 0.0)
+            nc.vector.memset(board[t][:].bitcast(I32), 0)
 
         def load_plane(plane, scales):
             for q in range(4):
-                nc.sync.dma_start(plane[32 * q : 32 * q + 4, :].bitcast(I32), scales[0, 4 * q : 4 * q + 4, :].bitcast(I32))
+                nc.sync.dma_start(plane[QUAD * q : QUAD * q + 4, :].bitcast(I32), scales[0, 4 * q : 4 * q + 4, :].bitcast(I32))
 
-        def load_plane_folded(queue, folded, scales):
+        def load_plane_folded(folded, scales):
             rows = scales[0].bitcast(I32).rearrange("(c h r) n -> h r c n", c=2, h=2)
             for h in range(2):
-                queue.dma_start(folded[32 * h : 32 * h + 4].bitcast(I32), rows[h])
+                nc.sync.dma_start(folded[QUAD * h : QUAD * h + 4].bitcast(I32), rows[h])
 
         def load_words(tab, words):
             nc.sync.dma_start(tab[:].bitcast(I32), words.bitcast(I32))
 
-        nc.sync.dma_start(idx[1][:], offs2)
-        nc.sync.dma_start(idx[0][:], offs)
+        nc.sync.dma_start(note_list[:], offs2)
         load_words(xo_tab, xo_words[0])
-        load_plane_folded(nc.sync, xo_fold, xo_scales)
+        nc.sync.dma_start(token_list[:], offs)
+        load_plane_folded(xo_fold, xo_scales)
         load_words(w0_raw, w0_words[0].rearrange("p n t -> p (n t)"))
-        load_plane_folded(nc.sync, w0sc_raw, w0_scales)
+        load_plane_folded(w0sc_fold, w0_scales)
         load_words(xt_tab, xt_words[0].rearrange("p n t -> p (n t)"))
         load_words(w_raw, w_words[0])
         load_plane(xt_sc, xt_scales)
-        load_plane_folded(nc.sync, wsc_raw, w_scales)
-        nc.sync.dma_start(idx[2][:], offs3)
-        nc.sync.dma_start(idx[3][:], offs4)
+        load_plane_folded(wsc_fold, w_scales)
+        nc.sync.dma_start(put_list[:], offs3)
+        nc.sync.dma_start(read_list[:], offs4)
         nc.sync.dma_start(sa_t[:], sa.rearrange("(p t) o -> p (t o)", t=PACK))
         load_words(wb_tab, wb_words[0].rearrange("p n t -> p (n t)"))
         load_plane(wb_sc, wb_scales)
-        nc.sync.dma_start(idx[4][:], offs5)
-        with nc.allow_non_contiguous_dma(reason="one value a partition and half"):
+        nc.sync.dma_start(floor_list[:], offs5)
+        with nc.allow_non_contiguous_dma(reason="one value a partition for each 128 output features"):
             nc.sync.dma_start(so_t[:], so.rearrange("(h p) o -> p (h o)", h=2))
         for h in range(2):
             nc.sync.dma_start(tz_tab[h][:], tz[h * P : (h + 1) * P, :])
@@ -103,46 +108,54 @@ def tile_list_boardownweighed_bank_one_stepfloor_kernel(
         wsc_t = [tile([P, P], U8, f"wsc_t{t}") for t in range(PACK)]
         acc = [psum.tile([P, J], F32, name=f"acc{t}") for t in range(PACK)]
 
-        nc.vector.tensor_copy(xo_g[:], xo_tab[:].indirect(idx[1][:]))
+        def dealt(dst, src, per_line):
+            return (dst.rearrange("p t (b i) -> p b t i", i=per_line), src.rearrange("p (b i t) -> p b t i", i=per_line, t=PACK))
+
+        def unfold_in_place(folded):
+            nc.vector.tensor_copy(folded[P // 2 : P, 0, :].bitcast(I32), folded[0 : P // 2, 1, :].bitcast(I32))
+
+        nc.vector.tensor_copy(xo_g[:], xo_tab[:].indirect(note_list[:]))
         for c in range(2):
-            nc.vector.tensor_copy(xo_sc[64 * c : 64 * c + 64, :].bitcast(I32), xo_fold[:, c, :].bitcast(I32))
-        nc.vector.tensor_copy(xo_gs[:], xo_sc[:].indirect(idx[1][:]))
-        nc.scalar.copy(w0_t[:].rearrange("p t (b i) -> p b t i", i=4), w0_raw[:].rearrange("p (b i t) -> p b t i", i=4, t=PACK))
-        nc.vector.tensor_copy(w0sc_raw[64:128, 0, :].bitcast(I32), w0sc_raw[0:64, 1, :].bitcast(I32))
-        nc.vector.tensor_copy(w0sc_t[:].rearrange("p t (b i) -> p b t i", i=16),
-                              w0sc_raw[:, 0, :].rearrange("p (b i t) -> p b t i", i=16, t=PACK))
+            nc.vector.tensor_copy(xo_sc[P // 2 * c : P // 2 * (c + 1), :].bitcast(I32), xo_fold[:, c, :].bitcast(I32))
+        nc.vector.tensor_copy(xo_gs[:], xo_sc[:].indirect(note_list[:]))
+        nc.scalar.copy(*dealt(w0_t[:], w0_raw[:], 4))
+        unfold_in_place(w0sc_fold)
+        nc.vector.tensor_copy(*dealt(w0sc_t[:], w0sc_fold[:, 0, :], 16))
         for t in range(PACK):
             nc.tensor.matmul_mx(acc[t][:], lhsT=w0_t[:, t, :].bitcast(E5M2), lhsT_scale=w0sc_t[:, t, :],
                                 rhs=xo_g[:].bitcast(E2M1), rhs_scale=xo_gs[:], start=True, stop=False)
 
-        nc.vector.tensor_copy(xt_g[:], xt_tab[:].indirect(idx[0][:]))
-        nc.vector.tensor_copy(xt_gs[:], xt_sc[:].indirect(idx[0][:]))
-        nc.scalar.copy(w_t[:].rearrange("p t (b i) -> p b t i", i=8), w_raw[:].rearrange("p (b i t) -> p b t i", i=8, t=PACK))
-        nc.vector.tensor_copy(wsc_raw[64:128, 0, :].bitcast(I32), wsc_raw[0:64, 1, :].bitcast(I32))
+        nc.vector.tensor_copy(xt_g[:], xt_tab[:].indirect(token_list[:]))
+        nc.vector.tensor_copy(xt_gs[:], xt_sc[:].indirect(token_list[:]))
+        nc.scalar.copy(*dealt(w_t[:], w_raw[:], 8))
+        unfold_in_place(wsc_fold)
         for t in range(PACK):
-            nc.vector.tensor_copy(wsc_t[t][:], wsc_raw[:, 0, :].rearrange("p (q t) -> p t q", t=PACK)[:, t, :])
+            nc.vector.tensor_copy(wsc_t[t][:], wsc_fold[:, 0, :].rearrange("p (q t) -> p t q", t=PACK)[:, t, :])
             nc.tensor.matmul_mx(acc[t][:], lhsT=w_t[:, t, :].bitcast(E2M1), lhsT_scale=wsc_t[t][:],
                                 rhs=xt_g[:].bitcast(E4M3), rhs_scale=xt_gs[:], start=False, stop=True)
 
-        a = [tile([P, J], F32, f"a{t}", tag={2: "vector_slot", 3: "scalar_slot"}.get(t)) for t in range(PACK)]
-        cut = 16 * SHARE
+        a = [tile([P, J], F32, f"a{t}", tag={SPLIT_SLICE: "after_split", SCALAR_SLICE: "after_scalar"}.get(t)) for t in range(PACK)]
+        cut = 16 * SCALAR_SHARE
         for t in range(PACK):
             nc.scalar.copy(a[t][:], acc[t][:])
-        for t in range(2):
-            nc.vector.tensor_copy(board[t][:].indirect(idx[2][:]), a[t][:])
-        nc.scalar.activation(board[2][:].indirect(idx[2][:, 0:SHARE]), a[2][:, 0:cut], ACT.Copy)
-        nc.vector.tensor_copy(board[2][:].indirect(idx[2][:, SHARE:COLS]), a[2][:, cut:J])
-        nc.scalar.activation(board[3][:].indirect(idx[2][:]), a[3][:], ACT.Copy)
-        read = tile([P, PACK, J], F32, "read", tag="scalar_slot")
-        for t in (0, 3, 1):
-            nc.scalar.activation(read[:, t, :], board[t][:].indirect(idx[3][:]), ACT.Copy, scale=sa_t[:, t : t + 1])
-        diff = tile([P, 2, PACK, HALF], F32, "diff", tag="vector_slot")
+        for t in range(SPLIT_SLICE):
+            nc.vector.tensor_copy(board[t][:].indirect(put_list[:]), a[t][:])
+        nc.scalar.activation(board[SPLIT_SLICE][:].indirect(put_list[:, 0:SCALAR_SHARE]), a[SPLIT_SLICE][:, 0:cut], ACT.Copy)
+        nc.vector.tensor_copy(board[SPLIT_SLICE][:].indirect(put_list[:, SCALAR_SHARE:LIST_COLS]), a[SPLIT_SLICE][:, cut:J])
+        nc.scalar.activation(board[SCALAR_SLICE][:].indirect(put_list[:]), a[SCALAR_SLICE][:], ACT.Copy)
+
+        by_completion = (0, SCALAR_SLICE, 1, SPLIT_SLICE)
+        read = tile([P, PACK, J], F32, "read", tag="after_scalar")
+        for t in by_completion[:-1]:
+            nc.scalar.activation(read[:, t, :], board[t][:].indirect(read_list[:]), ACT.Copy, scale=sa_t[:, t : t + 1])
+        diff = tile([P, 2, PACK, HALF], F32, "diff", tag="after_split")
         for u in range(2):
-            cols = slice(u * HALF, (u + 1) * HALF)
-            nc.scalar.activation(read[:, 2, cols], board[2][:].indirect(idx[3][:, 8 * u : 8 * u + 8]),
-                                 ACT.Copy, scale=sa_t[:, 2:3])
-            for t in (0, 3, 1, 2):
-                nc.vector.tensor_tensor(diff[:, u, t, :], read[:, t, cols], acc[t][:, cols], ALU.subtract)
+            slots = slice(u * HALF, (u + 1) * HALF)
+            half_list = read_list[:, u * LIST_COLS // 2 : (u + 1) * LIST_COLS // 2]
+            nc.scalar.activation(read[:, SPLIT_SLICE, slots], board[SPLIT_SLICE][:].indirect(half_list),
+                                 ACT.Copy, scale=sa_t[:, SPLIT_SLICE : SPLIT_SLICE + 1])
+            for t in by_completion:
+                nc.vector.tensor_tensor(diff[:, u, t, :], read[:, t, slots], acc[t][:, slots], ALU.subtract)
 
         prod = [psum.tile([P, J], F32, name=f"prod{h}") for h in range(2)]
         for u in range(2):
@@ -150,21 +163,21 @@ def tile_list_boardownweighed_bank_one_stepfloor_kernel(
             n_scalar = HALF if u == 0 else HALF - ABS_VECTOR
             nc.scalar.activation(hid[:, 0 : n_scalar * PACK].rearrange("p (c i t) -> p c t i", i=4, t=PACK),
                                  diff[:, u, :, 0:n_scalar].rearrange("p t (c i) -> p c t i", i=4), ACT.Abs)
-            if u == 1:
+            if n_scalar < HALF:
                 rest = diff[:, u, :, n_scalar:HALF].rearrange("p t j -> p j t")
                 nc.vector.scalar_tensor_tensor(hid[:, n_scalar * PACK :].rearrange("p (j t) -> p j t", t=PACK),
                                                rest, -1.0, rest, ALU.mult, ALU.max)
-            hq = tile([P, HALF], U32, f"hq{u}")
-            hs = tile([P, HALF], U8, f"hs{u}")
-            nc.vector.quantize_mx(hq[:].bitcast(E4M3), hs[:], hid[:])
+            hid_words = tile([P, HALF], U32, f"hid_words{u}")
+            hid_sc = tile([P, HALF], U8, f"hid_sc{u}")
+            nc.vector.quantize_mx(hid_words[:].bitcast(E4M3), hid_sc[:], hid[:])
             for h in range(2):
                 nc.tensor.matmul_mx(prod[h][:, u * HALF : (u + 1) * HALF], lhsT=wb_tab[:, h * P : (h + 1) * P].bitcast(E5M2),
-                                    lhsT_scale=wb_sc[:, h * P : (h + 1) * P], rhs=hq[:].bitcast(E4M3), rhs_scale=hs[:],
-                                    start=True, stop=True)
+                                    lhsT_scale=wb_sc[:, h * P : (h + 1) * P], rhs=hid_words[:].bitcast(E4M3),
+                                    rhs_scale=hid_sc[:], start=True, stop=True)
 
-        floor = tile([P, 2, J], F32, "floor", tag="vector_slot")
+        floor = tile([P, 2, J], F32, "floor", tag="after_split")
         for h in range(2):
-            nc.scalar.activation(floor[:, h, :], tz_tab[h][:].indirect(idx[4][:]), ACT.Copy, scale=so_t[:, h : h + 1])
+            nc.scalar.activation(floor[:, h, :], tz_tab[h][:].indirect(floor_list[:]), ACT.Copy, scale=so_t[:, h : h + 1])
             y = tile([P, J], F32, f"y{h}")
             nc.vector.tensor_tensor(y[:], prod[h][:], floor[:, h, :], ALU.max)
             nc.sync.dma_start(out[h * P : (h + 1) * P, :], y[:])

from contextlib import ExitStack

import concourse.mybir as mybir

K, F, T, Z, J, R, C, N, E = 512, 512, 1024, 1024, 256, 512, 512, 256, 1024
FLOPS = 2 * J * (K * R + F * R + R * N)

F32 = mybir.dt.float32
BF16 = mybir.dt.bfloat16
I32 = mybir.dt.int32
U32 = mybir.dt.uint32
U16 = mybir.dt.uint16
U8 = mybir.dt.uint8
E4M3 = mybir.dt.float8_e4m3fn_x4
E5M2 = mybir.dt.float8_e5m2_x4
E2M1 = mybir.dt.float4_e2m1fn_x4
ACT = mybir.ActivationFunctionType
ALU = mybir.AluOpType

P = 128
PACK = 4
QUAD = 32
HALF = J // 2
LIST_COLS = J // 16
SPLIT_SLICE = 2
SCALAR_SLICE = 3
SCALAR_SHARE = 4
ABS_VECTOR = 64


def tile_list_boardownweighed_bank_one_stepfloor_kernel(
    tc, xt_words, xt_scales, w_words, w_scales, xo_words, xo_scales, w0_words, w0_scales,
    sa, wb_words, wb_scales, tz, so, offs, offs2, offs3, offs4, offs5, out,
):
    nc = tc.nc
    with ExitStack() as ctx:
        lists = ctx.enter_context(tc.tile_pool(name="lists", bufs=1))
        sb = ctx.enter_context(tc.tile_pool(name="sb", bufs=1))
        psum = ctx.enter_context(tc.psum_pool(name="psum", bufs=1))

        def tile(shape, dtype, name, tag=None):
            return sb.tile(shape, dtype, name=name, tag=tag or name, align_bytes=64)

        token_list, note_list, put_list, read_list, floor_list = [
            lists.tile([P, LIST_COLS], U16, name=f"list{i}") for i in range(5)
        ]
        xt_tab = tile([P, T], U32, "xt_tab")
        xo_tab = tile([P, Z], U16, "xo_tab")
        xo_fold = tile([P // 2, 2, Z], U8, "xo_fold")
        xt_sc = tile([P, T], U8, "xt_sc")
        xo_sc = tile([P, Z], U8, "xo_sc")
        w_raw = tile([P, R], U16, "w_raw")
        w0_raw = tile([P, R], U32, "w0_raw")
        wsc_fold = tile([P, 2, R], U8, "wsc_fold")
        w0sc_fold = tile([P, 2, R], U8, "w0sc_fold")
        wb_tab = tile([P, N], U32, "wb_tab")
        wb_sc = tile([P, N], U8, "wb_sc")
        tz_tab = [tile([P, E], F32, f"tz{h}") for h in range(2)]
        sa_t = tile([P, PACK], F32, "sa_t")
        so_t = tile([P, 2], F32, "so_t")
        board = [tile([P, C], F32, f"board{t}") for t in range(PACK)]

        for plane in (xo_fold, w0sc_fold, xt_sc, wsc_fold, wb_sc):
            nc.vector.memset(plane[:].bitcast(I32), 0)
        for t in range(PACK):
            nc.vector.memset(board[t][:].bitcast(I32), 0)

        def load_plane(plane, scales):
            for q in range(4):
                nc.sync.dma_start(plane[QUAD * q : QUAD * q + 4, :].bitcast(I32), scales[0, 4 * q : 4 * q + 4, :].bitcast(I32))

        def load_plane_folded(folded, scales):
            rows = scales[0].bitcast(I32).rearrange("(c h r) n -> h r c n", c=2, h=2)
            for h in range(2):
                nc.sync.dma_start(folded[QUAD * h : QUAD * h + 4].bitcast(I32), rows[h])

        def load_words(tab, words):
            nc.sync.dma_start(tab[:].bitcast(I32), words.bitcast(I32))

        nc.sync.dma_start(note_list[:], offs2)
        load_words(xo_tab, xo_words[0])
        nc.sync.dma_start(token_list[:], offs)
        load_plane_folded(xo_fold, xo_scales)
        load_words(w0_raw, w0_words[0].rearrange("p n t -> p (n t)"))
        load_plane_folded(w0sc_fold, w0_scales)
        load_words(xt_tab, xt_words[0].rearrange("p n t -> p (n t)"))
        load_words(w_raw, w_words[0])
        load_plane(xt_sc, xt_scales)
        load_plane_folded(wsc_fold, w_scales)
        nc.sync.dma_start(put_list[:], offs3)
        nc.sync.dma_start(read_list[:], offs4)
        nc.sync.dma_start(sa_t[:], sa.rearrange("(p t) o -> p (t o)", t=PACK))
        load_words(wb_tab, wb_words[0].rearrange("p n t -> p (n t)"))
        load_plane(wb_sc, wb_scales)
        nc.sync.dma_start(floor_list[:], offs5)
        with nc.allow_non_contiguous_dma(reason="one value a partition for each 128 output features"):
            nc.sync.dma_start(so_t[:], so.rearrange("(h p) o -> p (h o)", h=2))
        for h in range(2):
            nc.sync.dma_start(tz_tab[h][:], tz[h * P : (h + 1) * P, :])

        xt_g = tile([P, J], U32, "xt_g")
        xt_gs = tile([P, J], U8, "xt_gs")
        xo_g = tile([P, J], U16, "xo_g")
        xo_gs = tile([P, J], U8, "xo_gs")
        w_t = tile([P, PACK, P], U16, "w_t")
        w0_t = tile([P, PACK, P], U32, "w0_t")
        w0sc_t = tile([P, PACK, P], U8, "w0sc_t")
        wsc_t = [tile([P, P], U8, f"wsc_t{t}") for t in range(PACK)]
        acc = [psum.tile([P, J], F32, name=f"acc{t}") for t in range(PACK)]

        def dealt(dst, src, per_line):
            return (dst.rearrange("p t (b i) -> p b t i", i=per_line), src.rearrange("p (b i t) -> p b t i", i=per_line, t=PACK))

        def unfold_in_place(folded):
            nc.vector.tensor_copy(folded[P // 2 : P, 0, :].bitcast(I32), folded[0 : P // 2, 1, :].bitcast(I32))

        nc.vector.tensor_copy(xo_g[:], xo_tab[:].indirect(note_list[:]))
        for c in range(2):
            nc.vector.tensor_copy(xo_sc[P // 2 * c : P // 2 * (c + 1), :].bitcast(I32), xo_fold[:, c, :].bitcast(I32))
        nc.vector.tensor_copy(xo_gs[:], xo_sc[:].indirect(note_list[:]))
        nc.scalar.copy(*dealt(w0_t[:], w0_raw[:], 4))
        unfold_in_place(w0sc_fold)
        nc.vector.tensor_copy(*dealt(w0sc_t[:], w0sc_fold[:, 0, :], 16))
        for t in range(PACK):
            nc.tensor.matmul_mx(acc[t][:], lhsT=w0_t[:, t, :].bitcast(E5M2), lhsT_scale=w0sc_t[:, t, :],
                                rhs=xo_g[:].bitcast(E2M1), rhs_scale=xo_gs[:], start=True, stop=False)

        nc.vector.tensor_copy(xt_g[:], xt_tab[:].indirect(token_list[:]))
        nc.vector.tensor_copy(xt_gs[:], xt_sc[:].indirect(token_list[:]))
        nc.scalar.copy(*dealt(w_t[:], w_raw[:], 8))
        unfold_in_place(wsc_fold)
        for t in range(PACK):
            nc.vector.tensor_copy(wsc_t[t][:], wsc_fold[:, 0, :].rearrange("p (q t) -> p t q", t=PACK)[:, t, :])
            nc.tensor.matmul_mx(acc[t][:], lhsT=w_t[:, t, :].bitcast(E2M1), lhsT_scale=wsc_t[t][:],
                                rhs=xt_g[:].bitcast(E4M3), rhs_scale=xt_gs[:], start=False, stop=True)

        a = [tile([P, J], F32, f"a{t}", tag={SPLIT_SLICE: "after_split", SCALAR_SLICE: "after_scalar"}.get(t)) for t in range(PACK)]
        cut = 16 * SCALAR_SHARE
        for t in range(PACK):
            nc.scalar.copy(a[t][:], acc[t][:])
        for t in range(SPLIT_SLICE):
            nc.vector.tensor_copy(board[t][:].indirect(put_list[:]), a[t][:])
        nc.scalar.activation(board[SPLIT_SLICE][:].indirect(put_list[:, 0:SCALAR_SHARE]), a[SPLIT_SLICE][:, 0:cut], ACT.Copy)
        nc.vector.tensor_copy(board[SPLIT_SLICE][:].indirect(put_list[:, SCALAR_SHARE:LIST_COLS]), a[SPLIT_SLICE][:, cut:J])
        nc.scalar.activation(board[SCALAR_SLICE][:].indirect(put_list[:]), a[SCALAR_SLICE][:], ACT.Copy)

        by_completion = (0, SCALAR_SLICE, 1, SPLIT_SLICE)
        read = tile([P, PACK, J], F32, "read", tag="after_scalar")
        for t in by_completion[:-1]:
            nc.scalar.activation(read[:, t, :], board[t][:].indirect(read_list[:]), ACT.Copy, scale=sa_t[:, t : t + 1])
        diff = tile([P, 2, PACK, HALF], F32, "diff", tag="after_split")
        for u in range(2):
            slots = slice(u * HALF, (u + 1) * HALF)
            half_list = read_list[:, u * LIST_COLS // 2 : (u + 1) * LIST_COLS // 2]
            nc.scalar.activation(read[:, SPLIT_SLICE, slots], board[SPLIT_SLICE][:].indirect(half_list),
                                 ACT.Copy, scale=sa_t[:, SPLIT_SLICE : SPLIT_SLICE + 1])
            for t in by_completion:
                nc.vector.tensor_tensor(diff[:, u, t, :], read[:, t, slots], acc[t][:, slots], ALU.subtract)

        prod = [psum.tile([P, J], F32, name=f"prod{h}") for h in range(2)]
        for u in range(2):
            hid = tile([P, HALF * PACK], BF16, f"hid{u}")
            n_scalar = HALF if u == 0 else HALF - ABS_VECTOR
            nc.scalar.activation(hid[:, 0 : n_scalar * PACK].rearrange("p (c i t) -> p c t i", i=4, t=PACK),
                                 diff[:, u, :, 0:n_scalar].rearrange("p t (c i) -> p c t i", i=4), ACT.Abs)
            if n_scalar < HALF:
                rest = diff[:, u, :, n_scalar:HALF].rearrange("p t j -> p j t")
                nc.vector.scalar_tensor_tensor(hid[:, n_scalar * PACK :].rearrange("p (j t) -> p j t", t=PACK),
                                               rest, -1.0, rest, ALU.mult, ALU.max)
            hid_words = tile([P, HALF], U32, f"hid_words{u}")
            hid_sc = tile([P, HALF], U8, f"hid_sc{u}")
            nc.vector.quantize_mx(hid_words[:].bitcast(E4M3), hid_sc[:], hid[:])
            for h in range(2):
                nc.tensor.matmul_mx(prod[h][:, u * HALF : (u + 1) * HALF], lhsT=wb_tab[:, h * P : (h + 1) * P].bitcast(E5M2),
                                    lhsT_scale=wb_sc[:, h * P : (h + 1) * P], rhs=hid_words[:].bitcast(E4M3),
                                    rhs_scale=hid_sc[:], start=True, stop=True)

        floor = tile([P, 2, J], F32, "floor", tag="after_split")
        for h in range(2):
            nc.scalar.activation(floor[:, h, :], tz_tab[h][:].indirect(floor_list[:]), ACT.Copy, scale=so_t[:, h : h + 1])
            y = tile([P, J], F32, f"y{h}")
            nc.vector.tensor_tensor(y[:], prod[h][:], floor[:, h, :], ALU.max)
            nc.sync.dma_start(out[h * P : (h + 1) * P, :], y[:])
